import numpy as np
import ml_dtypes


def mxq(x, axis, fmt="e4m3"):
    dtype, down = {"e4m3": (ml_dtypes.float8_e4m3fn, 7), "e5m2": (ml_dtypes.float8_e5m2, 14)}[fmt]
    v = np.moveaxis(np.asarray(x, np.float32).astype(ml_dtypes.bfloat16).astype(np.float64), axis, -1)
    blocks = v.reshape(v.shape[:-1] + (-1, 32))
    amax = np.abs(blocks).max(-1, keepdims=True)
    byte = np.maximum(np.where(amax > 0, np.frexp(amax)[1] - 1 + 127, 0) - down, 1)
    scale = np.exp2(byte - 127.0)
    codes = (blocks / scale).astype(np.float32).astype(dtype).astype(np.float64)
    return np.moveaxis((codes * scale).reshape(v.shape), -1, axis)


WIDE = False


def mx_kscale(k):
    if not WIDE:
        return np.ones(k)
    levels = np.array([10, -10, 5, -5, 0])
    if k % 512:
        return np.exp2(np.random.permutation(np.resize(levels, k // 32))).repeat(32)
    a = np.empty((k // 512, 16))
    for p in range(k // 512):
        a[p, :8] = np.random.permutation(np.resize(levels, 8))
        for g in range(8):
            far = levels[np.abs(levels - a[p, g]) >= 10]
            a[p, g + 8] = far[np.random.randint(len(far))]
    return np.exp2(a.ravel()).repeat(32)


def f64(x):
    return np.asarray(x).astype(np.float64)


def striped(idx):
    return np.tile(np.asarray(idx).reshape(-1, 16).T, (8, 1)).astype(np.uint16)


def unstriped(offs):
    return offs[:16].T.reshape(-1).astype(np.int64)


E2M1 = np.array([0.0, 0.5, 1.0, 1.5, 2.0, 3.0, 4.0, 6.0, -0.0, -0.5, -1.0, -1.5, -2.0, -3.0, -4.0, -6.0])


def pack_weight(w, fmt):
    k, n = w.shape
    w = f64(np.asarray(w, np.float32).astype(ml_dtypes.bfloat16)).reshape(k // 32, 32, n)
    amax = np.abs(w).max(1)
    if fmt == "e4m3":
        byte = np.frexp(amax)[1] - 1 + 127 - 7
    else:
        mant, ex = np.frexp(amax / 6.0)
        byte = np.where(mant > 0.5, ex, ex - 1) + 127
    byte = np.clip(np.where(amax > 0, byte, 1), 1, 254)
    scaled = (w * np.exp2(127.0 - byte)[:, None, :]).reshape(k, n).astype(np.float32)
    by_word = np.ascontiguousarray(scaled.reshape(k // 512, 128, 4, n).transpose(0, 1, 3, 2))
    if fmt == "e4m3":
        words = by_word.astype(ml_dtypes.float8_e4m3fn).view(np.uint8)
    else:
        c = by_word.astype(ml_dtypes.float4_e2m1fn).view(np.uint8) & 0xF
        words = (c[..., 0::2] | (c[..., 1::2] << 4)).reshape(k // 512, 128, 2 * n)
    return np.ascontiguousarray(words), np.ascontiguousarray(byte.astype(np.uint8).reshape(k // 512, 16, n))


def unpack_weight(words, scales, fmt):
    g, _, n = scales.shape
    words = np.ascontiguousarray(words).reshape(g, 128, n, -1)
    if fmt == "e4m3":
        vals = words.view(ml_dtypes.float8_e4m3fn).astype(np.float64)
    else:
        nib = np.empty((g, 128, n, 4), np.uint8)
        nib[..., 0::2] = words & 0xF
        nib[..., 1::2] = words >> 4
        vals = E2M1[nib]
    vals = vals * np.repeat(np.exp2(scales.astype(np.float64) - 127.0), 8, axis=1)[..., None]
    return vals.transpose(0, 1, 3, 2).reshape(g * 512, n)


D, T, I, G, F, Q = 512, 2048, 1024, 256, 512, 128


def setup_inputs():
    n = np.random.standard_normal
    idx = np.random.permutation(T)[:I]
    fd = mx_kscale(D)
    fi = mx_kscale(I)
    ti = np.ones(T)
    ti[idx] = fi
    sensep = pack_weight(n((D, T)) / fd[:, None], "e4m3")
    return {
        "hid": (n((D, Q)) * 0.8 / np.sqrt(D) * fd[:, None]).astype(np.float32),
        "sense_words": sensep[0],
        "sense_scales": sensep[1],
        "up": (0.1 * n((Q, G))).astype(np.float32),
        "fs": (np.random.uniform(0.5, 2.0, (1, I)) * fi).astype(np.float32),
        "srows": (n((F, T)) / ti).astype(np.float32),
        "res": (n((Q, F)) * 1.0).astype(np.float32),
        "offs": striped(idx),
    }


def reference(hid, sense_words, sense_scales, up, fs, srows, res, offs):
    idx = unstriped(offs)
    senseu = unpack_weight(sense_words, sense_scales, "e4m3")
    hidq = mxq(f64(hid), 0, "e4m3")
    senseidxg = senseu[:, idx]
    a = hidq.T @ senseidxg
    p = np.exp(a - np.max(a, axis=1, keepdims=True))
    r = f64(up) / p.reshape(Q, G, I // G).sum(axis=2)
    rr = np.repeat(r, I // G, axis=1)
    ds = p * rr * f64(fs)
    dt = ds.T
    st = f64(srows)[:, idx].T
    dtq = mxq(dt, 0, "e4m3")
    stq = mxq(st, 0, "e4m3")
    gh = dtq.T @ stq
    y = gh + f64(res)
    return y

@@ -1,0 +1,216 @@
+from contextlib import ExitStack
+
+import concourse.mybir as mybir
+from concourse.masks import make_identity
+
+D, T, I, G, F, Q = 512, 2048, 1024, 256, 512, 128
+FLOPS = 2 * Q * I * D + 2 * Q * I * F
+
+F32 = mybir.dt.float32
+BF16 = mybir.dt.bfloat16
+I32 = mybir.dt.int32
+U32 = mybir.dt.uint32
+U16 = mybir.dt.uint16
+U8 = mybir.dt.uint8
+FP8X4 = mybir.dt.float8_e4m3fn_x4
+ALU = mybir.AluOpType
+ACT = mybir.ActivationFunctionType
+AX = mybir.AxisListType
+
+P = 128
+PACK = 4
+K_PASS = P * PACK
+PASSES = I // K_PASS
+PLANES = F // P
+LIST_COLS = K_PASS // 16
+
+
+def tile_attend_gsenses_kernel(tc, hid, sense_words, sense_scales, up, fs, srows, res, offs, out):
+    nc = tc.nc
+    with ExitStack() as ctx:
+        sb = ctx.enter_context(tc.tile_pool(name="sb", bufs=1))
+        ps = ctx.enter_context(tc.psum_pool(name="ps", bufs=1))
+
+        def sbuf(name, shape, dtype, takes_over=None):
+            return sb.tile(shape, dtype, name=name, tag=takes_over or name, align_bytes=64)
+
+        offsets = sb.tile([P, I // 16], U16, name="offsets")
+        nc.sync.dma_start(offsets[:], offs)
+
+        scale_pool = sbuf("scale_pool", [P, T], U8)
+        nc.gpsimd.memset(scale_pool[:].bitcast(I32), 0)
+        hid_raw = sbuf("hid_raw", [P, PACK, Q], F32)
+        nc.sync.dma_start(hid_raw[:], hid.rearrange("(p j) q -> p j q", j=PACK))
+        for quad in range(4):
+            nc.sync.dma_start(
+                scale_pool[32 * quad : 32 * quad + 4, :].bitcast(I32),
+                sense_scales[0, 4 * quad : 4 * quad + 4, :].bitcast(I32),
+            )
+        word_pool = sbuf("word_pool", [P, T], I32)
+        nc.sync.dma_start(word_pool[:], sense_words[0].rearrange("p t r -> p (t r)").bitcast(I32))
+
+        halves = [sbuf("rows0_half%d" % h, [P, T // 2], F32) for h in range(2)]
+        for h in range(2):
+            nc.sync.dma_start(halves[h][:], srows[0:P, h * (T // 2) : (h + 1) * (T // 2)])
+        planes = {c: sbuf("rows%d" % c, [P, T], F32) for c in range(1, PLANES)}
+        for c in range(1, PLANES):
+            nc.sync.dma_start(planes[c][:], srows[c * P : (c + 1) * P, :])
+        up_sb = sbuf("up_sb", [P, G], F32)
+        fs_sb = sbuf("fs_sb", [P, PASSES, PACK], F32)
+        res_sb = sbuf("res_sb", [P, F], F32)
+        nc.sync.dma_start(fs_sb[:], fs[0].rearrange("(g p t) -> p g t", g=PASSES, t=PACK))
+        nc.sync.dma_start(up_sb[:], up)
+        nc.sync.dma_start(res_sb[:], res)
+
+        ident = sbuf("ident", [P, P], F32)
+        make_identity(nc, ident[:])
+
+        hid_bf = sbuf("hid_bf", [P, Q, PACK], BF16)
+        nc.scalar.copy(
+            out=hid_bf[:].rearrange("p (c i) t -> p c t i", i=4),
+            in_=hid_raw[:].rearrange("p t (c i) -> p c t i", i=4),
+        )
+        rows0_bf = sbuf("rows0_bf", [P, T], BF16)
+        for h in range(2):
+            nc.scalar.activation(out=rows0_bf[:, h * (T // 2) : (h + 1) * (T // 2)], in_=halves[h][:], func=ACT.Copy)
+
+        key_scales = sbuf("key_scales", [P, I], U8)
+        nc.vector.tensor_copy(key_scales[:], scale_pool[:].indirect(offsets[:]))
+        hid_codes = sbuf("hid_codes", [P, Q], U32)
+        hid_scales = sbuf("hid_scales", [P, Q], U8)
+        nc.vector.quantize_mx(
+            out=hid_codes[:].bitcast(FP8X4), scales=hid_scales[:], in_=hid_bf[:].rearrange("p q t -> p (q t)")
+        )
+        key_words = [sbuf("key_words%d" % g, [P, K_PASS], U32) for g in range(PASSES)]
+        for g in range(PASSES):
+            pass_offsets = offsets[:, g * LIST_COLS : (g + 1) * LIST_COLS]
+            nc.vector.tensor_copy(key_words[g][:], word_pool[:].bitcast(U32).indirect(pass_offsets))
+
+        scores = [ps.tile([P, K_PASS], F32, name="scores%d" % g, tag="bank%d" % g) for g in range(PASSES)]
+        for g in range(PASSES):
+            nc.tensor.matmul_mx(
+                out=scores[g][:],
+                lhsT=hid_codes[:].bitcast(FP8X4),
+                lhsT_scale=hid_scales[:],
+                rhs=key_words[g][:].bitcast(FP8X4),
+                rhs_scale=key_scales[:, g * K_PASS : (g + 1) * K_PASS],
+                start=True,
+                stop=True,
+            )
+        neg_max = [sbuf("neg_max%d" % g, [P, 1], F32) for g in range(PASSES)]
+        probs = [
+            sbuf("probs0", [P, PACK, P], F32, takes_over="rows0_half1"),
+            sbuf("probs1", [P, PACK, P], F32),
+        ]
+        for g in range(PASSES):
+            nc.vector.tensor_reduce(out=neg_max[g][:], in_=scores[g][:], axis=AX.X, op=ALU.max, negate=True)
+            nc.scalar.activation(
+                out=probs[g][:],
+                in_=scores[g][:].rearrange("q (s t) -> q t s", t=PACK),
+                func=ACT.Exp,
+                bias=neg_max[g][:],
+                scale=1.0,
+            )
+
+        word_bank = ps.tile([P, 2, PASSES, Q], F32, name="word_bank")
+        turned = []
+        for g in range(PASSES):
+            for t in range(PACK):
+                nc.tensor.matmul(
+                    word_bank[:, 1, g, :], probs[g][:, t, :], ident[:],
+                    start=(t == 0), stop=(t == PACK - 1), is_transpose=True,
+                )
+            turned.append(ps.tile([P, PACK, Q], F32, name="turned%d" % g, tag="bank%d" % g))
+            for t in range(PACK):
+                nc.tensor.transpose(turned[g][:, t, :], probs[g][:, t, :], ident[:])
+
+        gathered = [sbuf("gathered0", [P, I], BF16, takes_over="neg_max1"), sbuf("gathered1", [P, I], BF16, takes_over="key_words1")]
+        gathered.extend([sbuf("gathered%d" % c, [P, I], BF16) for c in range(2, PLANES)])
+        nc.scalar.activation(out=gathered[0][:], in_=rows0_bf[:].indirect(offsets[:]), func=ACT.Copy)
+        for c in range(1, PLANES):
+            nc.vector.tensor_copy(gathered[c][:], planes[c][:].indirect(offsets[:]))
+
+        root = sbuf("root", [P, PASSES, Q], F32)
+        guess = sbuf("guess", [P, PASSES, Q], F32)
+        nc.scalar.activation(out=root[:], in_=word_bank[:, 1], func=ACT.Abs_reciprocal_sqrt)
+        nc.scalar.activation(out=guess[:], in_=root[:], func=ACT.Square)
+        scaled = [sbuf("scaled%d" % g, [P, PACK, Q], F32) for g in range(PASSES)]
+        for g in range(PASSES):
+            for t in range(PACK):
+                nc.scalar.activation(out=scaled[g][:, t, :], in_=turned[g][:, t, :], func=ACT.Copy, scale=fs_sb[:, g, t : t + 1])
+
+        st_words = [
+            sbuf("st_words0", [P, 2, PASSES, P, 2], F32, takes_over="root"),
+            sbuf("st_words1", [P, 2, PASSES, P, 2], F32),
+        ]
+
+        def turn(c):
+            bank = ps.tile([P, PASSES, 2, P], F32, name="turn%d" % c)
+            words = gathered[c][:].bitcast(F32)
+            for g in range(PASSES):
+                for u in range(2):
+                    nc.tensor.transpose(bank[:, g, u, :], words[:, 256 * g + u : 256 * (g + 1) : 2], ident[:])
+            nc.scalar.copy(out=st_words[c // 2][:, c % 2], in_=bank[:].rearrange("p g u f -> p g f u"))
+
+        for c in (1, 0, 2):
+            turn(c)
+        for g in range(PASSES):
+            nc.tensor.transpose(word_bank[:, 0, g, :], up_sb[:, g * P : (g + 1) * P], ident[:])
+        turn(3)
+
+        newton = sbuf("newton", [P, 2, PASSES, Q], F32, takes_over="rows3")
+        nearly_one = newton[:, 0]
+        neg_share = newton[:, 1]
+        share = sbuf("share", [P, PASSES, Q], F32)
+        nc.vector.tensor_tensor(out=nearly_one, in0=word_bank[:, 1], in1=guess[:], op=ALU.mult)
+        nc.vector.scalar_tensor_tensor(
+            out=neg_share, in0=word_bank[:, 0], scalar=-1.0, in1=guess[:], op0=ALU.mult, op1=ALU.mult
+        )
+        nc.vector.scalar_tensor_tensor(
+            out=share[:], in0=nearly_one, scalar=2.0, in1=neg_share, op0=ALU.subtract, op1=ALU.mult
+        )
+        dt_bf = sbuf("dt_bf", [P, PASSES, Q, PACK], BF16)
+        for g in range(PASSES):
+            nc.vector.tensor_tensor(
+                out=dt_bf[:, g].rearrange("p (c i) t -> p c t i", i=4),
+                in0=scaled[g][:].rearrange("p t (c i) -> p c t i", i=4),
+                in1=share[:, g].rearrange("p (c i) -> p c i", i=4).unsqueeze(2).to_broadcast([P, Q // 4, PACK, 4]),
+                op=ALU.mult,
+            )
+        dt_codes = sbuf("dt_codes", [P, PASSES, Q], U32)
+        dt_scales = sbuf("dt_scales", [P, PASSES, Q], U8)
+        st_codes = [sbuf("st_codes%d" % h, [P, 2, PASSES, P], U32, takes_over="scaled%d" % h) for h in range(2)]
+        st_scales = [sbuf("st_scales%d" % h, [P, 2, PASSES, P], U8) for h in range(2)]
+
+        def quantize_rows(h):
+            nc.vector.quantize_mx(
+                out=st_codes[h][:].rearrange("p c g f -> p (c g f)").bitcast(FP8X4),
+                scales=st_scales[h][:].rearrange("p c g f -> p (c g f)"),
+                in_=st_words[h][:].rearrange("p c g f u -> p (c g f u)").bitcast(BF16),
+            )
+
+        quantize_rows(0)
+        nc.vector.quantize_mx(
+            out=dt_codes[:].rearrange("p g q -> p (g q)").bitcast(FP8X4),
+            scales=dt_scales[:].rearrange("p g q -> p (g q)"),
+            in_=dt_bf[:].rearrange("p g q t -> p (g q t)"),
+        )
+        quantize_rows(1)
+
+        for h in range(2):
+            acc = ps.tile([P, 2, P], F32, name="acc%d" % h, tag="bank%d" % h)
+            for c in range(2):
+                for g in range(PASSES):
+                    nc.tensor.matmul_mx(
+                        out=acc[:, c, :],
+                        lhsT=dt_codes[:, g].bitcast(FP8X4),
+                        lhsT_scale=dt_scales[:, g],
+                        rhs=st_codes[h][:, c, g].bitcast(FP8X4),
+                        rhs_scale=st_scales[h][:, c, g],
+                        start=(g == 0),
+                        stop=(g == PASSES - 1),
+                    )
+            cols = slice(h * 2 * P, (h + 1) * 2 * P)
+            result = sbuf("result%d" % h, [P, 2 * P], F32)
+            nc.vector.tensor_tensor(out=result[:], in0=acc[:].rearrange("p c f -> p (c f)"), in1=res_sb[:, cols], op=ALU.add)
+            nc.sync.dma_start(out[:, cols], result[:])

@@ -23,6 +23,8 @@ K_PASS = P * PACK
 PASSES = I // K_PASS
 PLANES = F // P
 LIST_COLS = K_PASS // 16
+SCALAR_PLANE = 2
+VECTOR_PLANES = (0, 1, 3)
 
 
 def tile_attend_gsenses_kernel(tc, hid, sense_words, sense_scales, up, fs, srows, res, offs, out):
@@ -46,33 +48,52 @@ def tile_attend_gsenses_kernel(tc, hid, sense_words, sense_scales, up, fs, srows
                 scale_pool[32 * quad : 32 * quad + 4, :].bitcast(I32),
                 sense_scales[0, 4 * quad : 4 * quad + 4, :].bitcast(I32),
             )
+        up_sb = sbuf("up_sb", [P, G], F32)
+        nc.sync.dma_start(up_sb[:], up)
         word_pool = sbuf("word_pool", [P, T], I32)
         nc.sync.dma_start(word_pool[:], sense_words[0].rearrange("p t r -> p (t r)").bitcast(I32))
 
-        halves = [sbuf("rows0_half%d" % h, [P, T // 2], F32) for h in range(2)]
+        halves = [sbuf("rows_half%d" % h, [P, T // 2], F32) for h in range(2)]
         for h in range(2):
-            nc.sync.dma_start(halves[h][:], srows[0:P, h * (T // 2) : (h + 1) * (T // 2)])
-        planes = {c: sbuf("rows%d" % c, [P, T], F32) for c in range(1, PLANES)}
-        for c in range(1, PLANES):
-            nc.sync.dma_start(planes[c][:], srows[c * P : (c + 1) * P, :])
-        up_sb = sbuf("up_sb", [P, G], F32)
+            nc.sync.dma_start(
+                halves[h][:], srows[SCALAR_PLANE * P : (SCALAR_PLANE + 1) * P, h * (T // 2) : (h + 1) * (T // 2)]
+            )
         fs_sb = sbuf("fs_sb", [P, PASSES, PACK], F32)
-        res_sb = sbuf("res_sb", [P, F], F32)
         nc.sync.dma_start(fs_sb[:], fs[0].rearrange("(g p t) -> p g t", g=PASSES, t=PACK))
-        nc.sync.dma_start(up_sb[:], up)
+        planes = {c: sbuf("rows%d" % c, [P, T], F32) for c in VECTOR_PLANES}
+        for c in VECTOR_PLANES:
+            nc.sync.dma_start(planes[c][:], srows[c * P : (c + 1) * P, :])
+        res_sb = sbuf("res_sb", [P, F], F32)
         nc.sync.dma_start(res_sb[:], res)
 
         ident = sbuf("ident", [P, P], F32)
         make_identity(nc, ident[:])
+
+        word_bank = ps.tile([P, 2, PASSES, Q], F32, name="word_bank")
+        for g in range(PASSES):
+            nc.tensor.transpose(word_bank[:, 0, g, :], up_sb[:, g * P : (g + 1) * P], ident[:])
 
         hid_bf = sbuf("hid_bf", [P, Q, PACK], BF16)
         nc.scalar.copy(
             out=hid_bf[:].rearrange("p (c i) t -> p c t i", i=4),
             in_=hid_raw[:].rearrange("p t (c i) -> p c t i", i=4),
         )
-        rows0_bf = sbuf("rows0_bf", [P, T], BF16)
+        rows_bf = sbuf("rows_bf", [P, T], BF16)
         for h in range(2):
-            nc.scalar.activation(out=rows0_bf[:, h * (T // 2) : (h + 1) * (T // 2)], in_=halves[h][:], func=ACT.Copy)
+            nc.scalar.activation(out=rows_bf[:, h * (T // 2) : (h + 1) * (T // 2)], in_=halves[h][:], func=ACT.Copy)
+
+        def slots(first, count):
+            return offsets[:, first // 16 : (first + count) // 16]
+
+        picked = {}
+
+        def gather_on_scalar(g, takes_over=None):
+            picked[SCALAR_PLANE, g] = sbuf("picked_scalar%d" % g, [P, K_PASS], BF16, takes_over)[:]
+            nc.scalar.activation(
+                out=picked[SCALAR_PLANE, g], in_=rows_bf[:].indirect(slots(g * K_PASS, K_PASS)), func=ACT.Copy
+            )
+
+        gather_on_scalar(0)
 
         key_scales = sbuf("key_scales", [P, I], U8)
         nc.vector.tensor_copy(key_scales[:], scale_pool[:].indirect(offsets[:]))
@@ -81,25 +102,23 @@ def tile_attend_gsenses_kernel(tc, hid, sense_words, sense_scales, up, fs, srows
         nc.vector.quantize_mx(
             out=hid_codes[:].bitcast(FP8X4), scales=hid_scales[:], in_=hid_bf[:].rearrange("p q t -> p (q t)")
         )
-        key_words = [sbuf("key_words%d" % g, [P, K_PASS], U32) for g in range(PASSES)]
-        for g in range(PASSES):
-            pass_offsets = offsets[:, g * LIST_COLS : (g + 1) * LIST_COLS]
-            nc.vector.tensor_copy(key_words[g][:], word_pool[:].bitcast(U32).indirect(pass_offsets))
-
         scores = [ps.tile([P, K_PASS], F32, name="scores%d" % g, tag="bank%d" % g) for g in range(PASSES)]
-        for g in range(PASSES):
+        for first, count in ((0, 512), (512, 256), (768, 256)):
+            key_words = sbuf("key_words%d" % first, [P, count], U32)
+            nc.vector.tensor_copy(key_words[:], word_pool[:].bitcast(U32).indirect(slots(first, count)))
+            g, col = divmod(first, K_PASS)
             nc.tensor.matmul_mx(
-                out=scores[g][:],
+                out=scores[g][:, col : col + count],
                 lhsT=hid_codes[:].bitcast(FP8X4),
                 lhsT_scale=hid_scales[:],
-                rhs=key_words[g][:].bitcast(FP8X4),
-                rhs_scale=key_scales[:, g * K_PASS : (g + 1) * K_PASS],
+                rhs=key_words[:].bitcast(FP8X4),
+                rhs_scale=key_scales[:, first : first + count],
                 start=True,
                 stop=True,
             )
         neg_max = [sbuf("neg_max%d" % g, [P, 1], F32) for g in range(PASSES)]
         probs = [
-            sbuf("probs0", [P, PACK, P], F32, takes_over="rows0_half1"),
+            sbuf("probs0", [P, PACK, P], F32, takes_over="rows_half1"),
             sbuf("probs1", [P, PACK, P], F32),
         ]
         for g in range(PASSES):
@@ -112,7 +131,7 @@ def tile_attend_gsenses_kernel(tc, hid, sense_words, sense_scales, up, fs, srows
                 scale=1.0,
             )
 
-        word_bank = ps.tile([P, 2, PASSES, Q], F32, name="word_bank")
+        gather_on_scalar(1, takes_over="neg_max1")
         turned = []
         for g in range(PASSES):
             for t in range(PACK):
@@ -120,55 +139,45 @@ def tile_attend_gsenses_kernel(tc, hid, sense_words, sense_scales, up, fs, srows
                     word_bank[:, 1, g, :], probs[g][:, t, :], ident[:],
                     start=(t == 0), stop=(t == PACK - 1), is_transpose=True,
                 )
-            turned.append(ps.tile([P, PACK, Q], F32, name="turned%d" % g, tag="bank%d" % g))
+            turned.append(ps.tile([P, PACK, Q], F32, name="turned%d" % g, tag=("bank2", "bank0")[g]))
             for t in range(PACK):
                 nc.tensor.transpose(turned[g][:, t, :], probs[g][:, t, :], ident[:])
 
-        gathered = [sbuf("gathered0", [P, I], BF16, takes_over="neg_max1"), sbuf("gathered1", [P, I], BF16, takes_over="key_words1")]
-        gathered.extend([sbuf("gathered%d" % c, [P, I], BF16) for c in range(2, PLANES)])
-        nc.scalar.activation(out=gathered[0][:], in_=rows0_bf[:].indirect(offsets[:]), func=ACT.Copy)
-        for c in range(1, PLANES):
-            nc.vector.tensor_copy(gathered[c][:], planes[c][:].indirect(offsets[:]))
+        for c in VECTOR_PLANES:
+            whole = sbuf("picked%d" % c, [P, I], BF16, takes_over="key_words768" if c == 0 else None)
+            nc.vector.tensor_copy(whole[:], planes[c][:].indirect(offsets[:]))
+            for g in range(PASSES):
+                picked[c, g] = whole[:, g * K_PASS : (g + 1) * K_PASS]
 
         root = sbuf("root", [P, PASSES, Q], F32)
         guess = sbuf("guess", [P, PASSES, Q], F32)
         nc.scalar.activation(out=root[:], in_=word_bank[:, 1], func=ACT.Abs_reciprocal_sqrt)
         nc.scalar.activation(out=guess[:], in_=root[:], func=ACT.Square)
-        scaled = [sbuf("scaled%d" % g, [P, PACK, Q], F32) for g in range(PASSES)]
+        scaled = [sbuf("scaled0", [P, PACK, Q], F32, takes_over="root"), sbuf("scaled1", [P, PACK, Q], F32)]
         for g in range(PASSES):
             for t in range(PACK):
                 nc.scalar.activation(out=scaled[g][:, t, :], in_=turned[g][:, t, :], func=ACT.Copy, scale=fs_sb[:, g, t : t + 1])
 
-        st_words = [
-            sbuf("st_words0", [P, 2, PASSES, P, 2], F32, takes_over="root"),
-            sbuf("st_words1", [P, 2, PASSES, P, 2], F32),
-        ]
+        turned_rows = {}
 
         def turn(c):
-            bank = ps.tile([P, PASSES, 2, P], F32, name="turn%d" % c)
-            words = gathered[c][:].bitcast(F32)
+            bank = ps.tile([P, PASSES, 2, P], F32, name="turn%d" % c, tag="bank1" if c == 0 else "turn%d" % c)
             for g in range(PASSES):
+                words = picked[c, g].bitcast(F32)
                 for u in range(2):
-                    nc.tensor.transpose(bank[:, g, u, :], words[:, 256 * g + u : 256 * (g + 1) : 2], ident[:])
-            nc.scalar.copy(out=st_words[c // 2][:, c % 2], in_=bank[:].rearrange("p g u f -> p g f u"))
+                    nc.tensor.transpose(bank[:, g, u, :], words[:, u::2], ident[:])
+            turned_rows[c] = bank[:].rearrange("p g u f -> p g f u")
 
-        for c in (1, 0, 2):
+        for c in range(PLANES):
             turn(c)
-        for g in range(PASSES):
-            nc.tensor.transpose(word_bank[:, 0, g, :], up_sb[:, g * P : (g + 1) * P], ident[:])
-        turn(3)
+        st_pair = sbuf("st_pair", [P, 2, PASSES, P, 2], F32, takes_over="fs_sb")
+        for c in range(2):
+            nc.scalar.copy(out=st_pair[:, c], in_=turned_rows[c])
+        st_third = sbuf("st_third", [P, PASSES, P, 2], F32, takes_over="guess")
+        nc.scalar.copy(out=st_third[:], in_=turned_rows[2])
 
-        newton = sbuf("newton", [P, 2, PASSES, Q], F32, takes_over="rows3")
-        nearly_one = newton[:, 0]
-        neg_share = newton[:, 1]
-        share = sbuf("share", [P, PASSES, Q], F32)
-        nc.vector.tensor_tensor(out=nearly_one, in0=word_bank[:, 1], in1=guess[:], op=ALU.mult)
-        nc.vector.scalar_tensor_tensor(
-            out=neg_share, in0=word_bank[:, 0], scalar=-1.0, in1=guess[:], op0=ALU.mult, op1=ALU.mult
-        )
-        nc.vector.scalar_tensor_tensor(
-            out=share[:], in0=nearly_one, scalar=2.0, in1=neg_share, op0=ALU.subtract, op1=ALU.mult
-        )
+        share = sbuf("share", [P, PASSES, Q], F32, takes_over="rows3")
+        nc.vector.tensor_tensor(out=share[:], in0=word_bank[:, 0], in1=guess[:], op=ALU.mult)
         dt_bf = sbuf("dt_bf", [P, PASSES, Q, PACK], BF16)
         for g in range(PASSES):
             nc.vector.tensor_tensor(
@@ -177,28 +186,31 @@ def tile_attend_gsenses_kernel(tc, hid, sense_words, sense_scales, up, fs, srows
                 in1=share[:, g].rearrange("p (c i) -> p c i", i=4).unsqueeze(2).to_broadcast([P, Q // 4, PACK, 4]),
                 op=ALU.mult,
             )
+        st_last = sbuf("st_last", [P, PASSES, P, 2], F32, takes_over="scaled1")
+        nc.vector.tensor_copy(out=st_last[:], in_=turned_rows[3])
         dt_codes = sbuf("dt_codes", [P, PASSES, Q], U32)
         dt_scales = sbuf("dt_scales", [P, PASSES, Q], U8)
-        st_codes = [sbuf("st_codes%d" % h, [P, 2, PASSES, P], U32, takes_over="scaled%d" % h) for h in range(2)]
-        st_scales = [sbuf("st_scales%d" % h, [P, 2, PASSES, P], U8) for h in range(2)]
-
-        def quantize_rows(h):
-            nc.vector.quantize_mx(
-                out=st_codes[h][:].rearrange("p c g f -> p (c g f)").bitcast(FP8X4),
-                scales=st_scales[h][:].rearrange("p c g f -> p (c g f)"),
-                in_=st_words[h][:].rearrange("p c g f u -> p (c g f u)").bitcast(BF16),
-            )
-
-        quantize_rows(0)
         nc.vector.quantize_mx(
             out=dt_codes[:].rearrange("p g q -> p (g q)").bitcast(FP8X4),
             scales=dt_scales[:].rearrange("p g q -> p (g q)"),
             in_=dt_bf[:].rearrange("p g q t -> p (g q t)"),
         )
-        quantize_rows(1)
+        st_codes = [sbuf("st_codes%d" % h, [P, 2, PASSES, P], U32, takes_over=("rows3", "dt_bf")[h]) for h in range(2)]
+        st_scales = [sbuf("st_scales%d" % h, [P, 2, PASSES, P], U8) for h in range(2)]
+        nc.vector.quantize_mx(
+            out=st_codes[0][:].rearrange("p c g f -> p (c g f)").bitcast(FP8X4),
+            scales=st_scales[0][:].rearrange("p c g f -> p (c g f)"),
+            in_=st_pair[:].rearrange("p c g f u -> p (c g f u)").bitcast(BF16),
+        )
+        for c, words in ((1, st_last), (0, st_third)):
+            nc.vector.quantize_mx(
+                out=st_codes[1][:, c].rearrange("p g f -> p (g f)").bitcast(FP8X4),
+                scales=st_scales[1][:, c].rearrange("p g f -> p (g f)"),
+                in_=words[:].rearrange("p g f u -> p (g f u)").bitcast(BF16),
+            )
 
         for h in range(2):
-            acc = ps.tile([P, 2, P], F32, name="acc%d" % h, tag="bank%d" % h)
+            acc = ps.tile([P, 2, P], F32, name="acc%d" % h, tag=("bank2", "bank0")[h])
             for c in range(2):
                 for g in range(PASSES):
                     nc.tensor.matmul_mx(

@@ -69,7 +69,7 @@ def tile_attend_gsenses_kernel(tc, hid, sense_words, sense_scales, up, fs, srows
         ident = sbuf("ident", [P, P], F32)
         make_identity(nc, ident[:])
 
-        word_bank = ps.tile([P, 2, PASSES, Q], F32, name="word_bank")
+        word_bank = ps.tile([P, 2, PASSES, Q], F32, name="word_bank", tag="word_bank")
         for g in range(PASSES):
             nc.tensor.transpose(word_bank[:, 0, g, :], up_sb[:, g * P : (g + 1) * P], ident[:])
 
@@ -119,7 +119,7 @@ def tile_attend_gsenses_kernel(tc, hid, sense_words, sense_scales, up, fs, srows
         neg_max = [sbuf("neg_max%d" % g, [P, 1], F32) for g in range(PASSES)]
         probs = [
             sbuf("probs0", [P, PACK, P], F32, takes_over="rows_half1"),
-            sbuf("probs1", [P, PACK, P], F32),
+            sbuf("probs1", [P, PACK, P], F32, takes_over="neg_max0"),
         ]
         for g in range(PASSES):
             nc.vector.tensor_reduce(out=neg_max[g][:], in_=scores[g][:], axis=AX.X, op=ALU.max, negate=True)
@@ -139,6 +139,7 @@ def tile_attend_gsenses_kernel(tc, hid, sense_words, sense_scales, up, fs, srows
                     word_bank[:, 1, g, :], probs[g][:, t, :], ident[:],
                     start=(t == 0), stop=(t == PACK - 1), is_transpose=True,
                 )
+        for g in range(PASSES):
             turned.append(ps.tile([P, PACK, Q], F32, name="turned%d" % g, tag=("bank2", "bank0")[g]))
             for t in range(PACK):
                 nc.tensor.transpose(turned[g][:, t, :], probs[g][:, t, :], ident[:])
@@ -153,76 +154,70 @@ def tile_attend_gsenses_kernel(tc, hid, sense_words, sense_scales, up, fs, srows
         guess = sbuf("guess", [P, PASSES, Q], F32)
         nc.scalar.activation(out=root[:], in_=word_bank[:, 1], func=ACT.Abs_reciprocal_sqrt)
         nc.scalar.activation(out=guess[:], in_=root[:], func=ACT.Square)
-        scaled = [sbuf("scaled0", [P, PACK, Q], F32, takes_over="root"), sbuf("scaled1", [P, PACK, Q], F32)]
+        scaled = sbuf("scaled", [P, PASSES, PACK, Q], F32, takes_over="root")
         for g in range(PASSES):
             for t in range(PACK):
-                nc.scalar.activation(out=scaled[g][:, t, :], in_=turned[g][:, t, :], func=ACT.Copy, scale=fs_sb[:, g, t : t + 1])
+                nc.scalar.activation(out=scaled[:, g, t, :], in_=turned[g][:, t, :], func=ACT.Copy, scale=fs_sb[:, g, t : t + 1])
 
-        turned_rows = {}
+        share = sbuf("share", [P, PASSES, Q], F32, takes_over="rows3")
+        nc.vector.tensor_tensor(out=share[:], in0=word_bank[:, 0], in1=guess[:], op=ALU.mult)
+        st_words = [
+            sbuf("st_words0", [P, PASSES, 2, P, 2], F32, takes_over="fs_sb"),
+            sbuf("st_words1", [P, PASSES, 2, P, 2], F32),
+        ]
 
         def turn(c):
-            bank = ps.tile([P, PASSES, 2, P], F32, name="turn%d" % c, tag="bank1" if c == 0 else "turn%d" % c)
+            bank = ps.tile([P, PASSES, 2, P], F32, name="turn%d" % c, tag=("bank2", "bank0", "word_bank", "bank2")[c])
             for g in range(PASSES):
                 words = picked[c, g].bitcast(F32)
                 for u in range(2):
                     nc.tensor.transpose(bank[:, g, u, :], words[:, u::2], ident[:])
-            turned_rows[c] = bank[:].rearrange("p g u f -> p g f u")
+            nc.scalar.copy(out=st_words[c // 2][:, :, c % 2], in_=bank[:].rearrange("p g u f -> p g f u"))
 
         for c in range(PLANES):
             turn(c)
-        st_pair = sbuf("st_pair", [P, 2, PASSES, P, 2], F32, takes_over="fs_sb")
-        for c in range(2):
-            nc.scalar.copy(out=st_pair[:, c], in_=turned_rows[c])
-        st_third = sbuf("st_third", [P, PASSES, P, 2], F32, takes_over="guess")
-        nc.scalar.copy(out=st_third[:], in_=turned_rows[2])
 
-        share = sbuf("share", [P, PASSES, Q], F32, takes_over="rows3")
-        nc.vector.tensor_tensor(out=share[:], in0=word_bank[:, 0], in1=guess[:], op=ALU.mult)
         dt_bf = sbuf("dt_bf", [P, PASSES, Q, PACK], BF16)
         for g in range(PASSES):
             nc.vector.tensor_tensor(
                 out=dt_bf[:, g].rearrange("p (c i) t -> p c t i", i=4),
-                in0=scaled[g][:].rearrange("p t (c i) -> p c t i", i=4),
+                in0=scaled[:, g].rearrange("p t (c i) -> p c t i", i=4),
                 in1=share[:, g].rearrange("p (c i) -> p c i", i=4).unsqueeze(2).to_broadcast([P, Q // 4, PACK, 4]),
                 op=ALU.mult,
             )
-        st_last = sbuf("st_last", [P, PASSES, P, 2], F32, takes_over="scaled1")
-        nc.vector.tensor_copy(out=st_last[:], in_=turned_rows[3])
         dt_codes = sbuf("dt_codes", [P, PASSES, Q], U32)
         dt_scales = sbuf("dt_scales", [P, PASSES, Q], U8)
+        st_codes = [sbuf("st_codes%d" % h, [P, PASSES, 2 * P], U32, takes_over=("root", "dt_bf")[h]) for h in range(2)]
+        st_scales = [sbuf("st_scales%d" % h, [P, PASSES, 2 * P], U8) for h in range(2)]
+
+        def quantize_rows(h):
+            nc.vector.quantize_mx(
+                out=st_codes[h][:].rearrange("p g f -> p (g f)").bitcast(FP8X4),
+                scales=st_scales[h][:].rearrange("p g f -> p (g f)"),
+                in_=st_words[h][:].rearrange("p g c f u -> p (g c f u)").bitcast(BF16),
+            )
+
+        quantize_rows(0)
         nc.vector.quantize_mx(
             out=dt_codes[:].rearrange("p g q -> p (g q)").bitcast(FP8X4),
             scales=dt_scales[:].rearrange("p g q -> p (g q)"),
             in_=dt_bf[:].rearrange("p g q t -> p (g q t)"),
         )
-        st_codes = [sbuf("st_codes%d" % h, [P, 2, PASSES, P], U32, takes_over=("rows3", "dt_bf")[h]) for h in range(2)]
-        st_scales = [sbuf("st_scales%d" % h, [P, 2, PASSES, P], U8) for h in range(2)]
-        nc.vector.quantize_mx(
-            out=st_codes[0][:].rearrange("p c g f -> p (c g f)").bitcast(FP8X4),
-            scales=st_scales[0][:].rearrange("p c g f -> p (c g f)"),
-            in_=st_pair[:].rearrange("p c g f u -> p (c g f u)").bitcast(BF16),
-        )
-        for c, words in ((1, st_last), (0, st_third)):
-            nc.vector.quantize_mx(
-                out=st_codes[1][:, c].rearrange("p g f -> p (g f)").bitcast(FP8X4),
-                scales=st_scales[1][:, c].rearrange("p g f -> p (g f)"),
-                in_=words[:].rearrange("p g f u -> p (g f u)").bitcast(BF16),
-            )
+        quantize_rows(1)
 
         for h in range(2):
-            acc = ps.tile([P, 2, P], F32, name="acc%d" % h, tag=("bank2", "bank0")[h])
-            for c in range(2):
-                for g in range(PASSES):
-                    nc.tensor.matmul_mx(
-                        out=acc[:, c, :],
-                        lhsT=dt_codes[:, g].bitcast(FP8X4),
-                        lhsT_scale=dt_scales[:, g],
-                        rhs=st_codes[h][:, c, g].bitcast(FP8X4),
-                        rhs_scale=st_scales[h][:, c, g],
-                        start=(g == 0),
-                        stop=(g == PASSES - 1),
-                    )
+            acc = ps.tile([P, 2 * P], F32, name="acc%d" % h)
+            for g in range(PASSES):
+                nc.tensor.matmul_mx(
+                    out=acc[:],
+                    lhsT=dt_codes[:, g].bitcast(FP8X4),
+                    lhsT_scale=dt_scales[:, g],
+                    rhs=st_codes[h][:, g].bitcast(FP8X4),
+                    rhs_scale=st_scales[h][:, g],
+                    start=(g == 0),
+                    stop=(g == PASSES - 1),
+                )
             cols = slice(h * 2 * P, (h + 1) * 2 * P)
             result = sbuf("result%d" % h, [P, 2 * P], F32)
-            nc.vector.tensor_tensor(out=result[:], in0=acc[:].rearrange("p c f -> p (c f)"), in1=res_sb[:, cols], op=ALU.add)
+            nc.vector.tensor_tensor(out=result[:], in0=acc[:], in1=res_sb[:, cols], op=ALU.add)
             nc.sync.dma_start(out[:, cols], result[:])

@@ -163,11 +163,11 @@ def tile_attend_gsenses_kernel(tc, hid, sense_words, sense_scales, up, fs, srows
         nc.vector.tensor_tensor(out=share[:], in0=word_bank[:, 0], in1=guess[:], op=ALU.mult)
         st_words = [
             sbuf("st_words0", [P, PASSES, 2, P, 2], F32, takes_over="fs_sb"),
-            sbuf("st_words1", [P, PASSES, 2, P, 2], F32),
+            sbuf("st_words1", [P, PASSES, 2, P, 2], F32, takes_over="guess"),
         ]
 
         def turn(c):
-            bank = ps.tile([P, PASSES, 2, P], F32, name="turn%d" % c, tag=("bank2", "bank0", "word_bank", "bank2")[c])
+            bank = ps.tile([P, PASSES, 2, P], F32, name="turn%d" % c, tag="bank1" if c == 0 else "turn%d" % c)
             for g in range(PASSES):
                 words = picked[c, g].bitcast(F32)
                 for u in range(2):
@@ -206,7 +206,7 @@ def tile_attend_gsenses_kernel(tc, hid, sense_words, sense_scales, up, fs, srows
         quantize_rows(1)
 
         for h in range(2):
-            acc = ps.tile([P, 2 * P], F32, name="acc%d" % h)
+            acc = ps.tile([P, 2 * P], F32, name="acc%d" % h, tag=("bank2", "bank0")[h])
             for g in range(PASSES):
                 nc.tensor.matmul_mx(
                     out=acc[:],

from contextlib import ExitStack

import concourse.mybir as mybir
from concourse.masks import make_identity

D, T, I, G, F, Q = 512, 2048, 1024, 256, 512, 128
FLOPS = 2 * Q * I * D + 2 * Q * I * F

F32 = mybir.dt.float32
BF16 = mybir.dt.bfloat16
I32 = mybir.dt.int32
U32 = mybir.dt.uint32
U16 = mybir.dt.uint16
U8 = mybir.dt.uint8
FP8X4 = mybir.dt.float8_e4m3fn_x4
ALU = mybir.AluOpType
ACT = mybir.ActivationFunctionType
AX = mybir.AxisListType

P = 128
PACK = 4
K_PASS = P * PACK
PASSES = I // K_PASS
PLANES = F // P
LIST_COLS = K_PASS // 16
SCALAR_PLANE = 2
VECTOR_PLANES = (0, 1, 3)


def tile_attend_gsenses_kernel(tc, hid, sense_words, sense_scales, up, fs, srows, res, offs, out):
    nc = tc.nc
    with ExitStack() as ctx:
        sb = ctx.enter_context(tc.tile_pool(name="sb", bufs=1))
        ps = ctx.enter_context(tc.psum_pool(name="ps", bufs=1))

        def sbuf(name, shape, dtype, takes_over=None):
            return sb.tile(shape, dtype, name=name, tag=takes_over or name, align_bytes=64)

        offsets = sb.tile([P, I // 16], U16, name="offsets")
        nc.sync.dma_start(offsets[:], offs)

        scale_pool = sbuf("scale_pool", [P, T], U8)
        nc.gpsimd.memset(scale_pool[:].bitcast(I32), 0)
        hid_raw = sbuf("hid_raw", [P, PACK, Q], F32)
        nc.sync.dma_start(hid_raw[:], hid.rearrange("(p j) q -> p j q", j=PACK))
        for quad in range(4):
            nc.sync.dma_start(
                scale_pool[32 * quad : 32 * quad + 4, :].bitcast(I32),
                sense_scales[0, 4 * quad : 4 * quad + 4, :].bitcast(I32),
            )
        up_sb = sbuf("up_sb", [P, G], F32)
        nc.sync.dma_start(up_sb[:], up)
        word_pool = sbuf("word_pool", [P, T], I32)
        nc.sync.dma_start(word_pool[:], sense_words[0].rearrange("p t r -> p (t r)").bitcast(I32))

        halves = [sbuf("rows_half%d" % h, [P, T // 2], F32) for h in range(2)]
        for h in range(2):
            nc.sync.dma_start(
                halves[h][:], srows[SCALAR_PLANE * P : (SCALAR_PLANE + 1) * P, h * (T // 2) : (h + 1) * (T // 2)]
            )
        fs_sb = sbuf("fs_sb", [P, PASSES, PACK], F32)
        nc.sync.dma_start(fs_sb[:], fs[0].rearrange("(g p t) -> p g t", g=PASSES, t=PACK))
        planes = {c: sbuf("rows%d" % c, [P, T], F32) for c in VECTOR_PLANES}
        for c in VECTOR_PLANES:
            nc.sync.dma_start(planes[c][:], srows[c * P : (c + 1) * P, :])
        res_sb = sbuf("res_sb", [P, F], F32)
        nc.sync.dma_start(res_sb[:], res)

        ident = sbuf("ident", [P, P], F32)
        make_identity(nc, ident[:])

        word_bank = ps.tile([P, 2, PASSES, Q], F32, name="word_bank", tag="word_bank")
        for g in range(PASSES):
            nc.tensor.transpose(word_bank[:, 0, g, :], up_sb[:, g * P : (g + 1) * P], ident[:])

        hid_bf = sbuf("hid_bf", [P, Q, PACK], BF16)
        nc.scalar.copy(
            out=hid_bf[:].rearrange("p (c i) t -> p c t i", i=4),
            in_=hid_raw[:].rearrange("p t (c i) -> p c t i", i=4),
        )
        rows_bf = sbuf("rows_bf", [P, T], BF16)
        for h in range(2):
            nc.scalar.activation(out=rows_bf[:, h * (T // 2) : (h + 1) * (T // 2)], in_=halves[h][:], func=ACT.Copy)

        def slots(first, count):
            return offsets[:, first // 16 : (first + count) // 16]

        picked = {}

        def gather_on_scalar(g, takes_over=None):
            picked[SCALAR_PLANE, g] = sbuf("picked_scalar%d" % g, [P, K_PASS], BF16, takes_over)[:]
            nc.scalar.activation(
                out=picked[SCALAR_PLANE, g], in_=rows_bf[:].indirect(slots(g * K_PASS, K_PASS)), func=ACT.Copy
            )

        gather_on_scalar(0)

        key_scales = sbuf("key_scales", [P, I], U8)
        nc.vector.tensor_copy(key_scales[:], scale_pool[:].indirect(offsets[:]))
        hid_codes = sbuf("hid_codes", [P, Q], U32)
        hid_scales = sbuf("hid_scales", [P, Q], U8)
        nc.vector.quantize_mx(
            out=hid_codes[:].bitcast(FP8X4), scales=hid_scales[:], in_=hid_bf[:].rearrange("p q t -> p (q t)")
        )
        scores = [ps.tile([P, K_PASS], F32, name="scores%d" % g, tag="bank%d" % g) for g in range(PASSES)]
        for first, count in ((0, 512), (512, 256), (768, 256)):
            key_words = sbuf("key_words%d" % first, [P, count], U32)
            nc.vector.tensor_copy(key_words[:], word_pool[:].bitcast(U32).indirect(slots(first, count)))
            g, col = divmod(first, K_PASS)
            nc.tensor.matmul_mx(
                out=scores[g][:, col : col + count],
                lhsT=hid_codes[:].bitcast(FP8X4),
                lhsT_scale=hid_scales[:],
                rhs=key_words[:].bitcast(FP8X4),
                rhs_scale=key_scales[:, first : first + count],
                start=True,
                stop=True,
            )
        neg_max = [sbuf("neg_max%d" % g, [P, 1], F32) for g in range(PASSES)]
        probs = [
            sbuf("probs0", [P, PACK, P], F32, takes_over="rows_half1"),
            sbuf("probs1", [P, PACK, P], F32, takes_over="neg_max0"),
        ]
        for g in range(PASSES):
            nc.vector.tensor_reduce(out=neg_max[g][:], in_=scores[g][:], axis=AX.X, op=ALU.max, negate=True)
            nc.scalar.activation(
                out=probs[g][:],
                in_=scores[g][:].rearrange("q (s t) -> q t s", t=PACK),
                func=ACT.Exp,
                bias=neg_max[g][:],
                scale=1.0,
            )

        gather_on_scalar(1, takes_over="neg_max1")
        turned = []
        for g in range(PASSES):
            for t in range(PACK):
                nc.tensor.matmul(
                    word_bank[:, 1, g, :], probs[g][:, t, :], ident[:],
                    start=(t == 0), stop=(t == PACK - 1), is_transpose=True,
                )
        for g in range(PASSES):
            turned.append(ps.tile([P, PACK, Q], F32, name="turned%d" % g, tag=("bank2", "bank0")[g]))
            for t in range(PACK):
                nc.tensor.transpose(turned[g][:, t, :], probs[g][:, t, :], ident[:])

        for c in VECTOR_PLANES:
            whole = sbuf("picked%d" % c, [P, I], BF16, takes_over="key_words768" if c == 0 else None)
            nc.vector.tensor_copy(whole[:], planes[c][:].indirect(offsets[:]))
            for g in range(PASSES):
                picked[c, g] = whole[:, g * K_PASS : (g + 1) * K_PASS]

        root = sbuf("root", [P, PASSES, Q], F32)
        guess = sbuf("guess", [P, PASSES, Q], F32)
        nc.scalar.activation(out=root[:], in_=word_bank[:, 1], func=ACT.Abs_reciprocal_sqrt)
        nc.scalar.activation(out=guess[:], in_=root[:], func=ACT.Square)
        scaled = sbuf("scaled", [P, PASSES, PACK, Q], F32, takes_over="root")
        for g in range(PASSES):
            for t in range(PACK):
                nc.scalar.activation(out=scaled[:, g, t, :], in_=turned[g][:, t, :], func=ACT.Copy, scale=fs_sb[:, g, t : t + 1])

        share = sbuf("share", [P, PASSES, Q], F32, takes_over="rows3")
        nc.vector.tensor_tensor(out=share[:], in0=word_bank[:, 0], in1=guess[:], op=ALU.mult)
        st_words = [
            sbuf("st_words0", [P, PASSES, 2, P, 2], F32, takes_over="fs_sb"),
            sbuf("st_words1", [P, PASSES, 2, P, 2], F32, takes_over="guess"),
        ]

        def turn(c):
            bank = ps.tile([P, PASSES, 2, P], F32, name="turn%d" % c, tag="bank1" if c == 0 else "turn%d" % c)
            for g in range(PASSES):
                words = picked[c, g].bitcast(F32)
                for u in range(2):
                    nc.tensor.transpose(bank[:, g, u, :], words[:, u::2], ident[:])
            nc.scalar.copy(out=st_words[c // 2][:, :, c % 2], in_=bank[:].rearrange("p g u f -> p g f u"))

        for c in range(PLANES):
            turn(c)

        dt_bf = sbuf("dt_bf", [P, PASSES, Q, PACK], BF16)
        for g in range(PASSES):
            nc.vector.tensor_tensor(
                out=dt_bf[:, g].rearrange("p (c i) t -> p c t i", i=4),
                in0=scaled[:, g].rearrange("p t (c i) -> p c t i", i=4),
                in1=share[:, g].rearrange("p (c i) -> p c i", i=4).unsqueeze(2).to_broadcast([P, Q // 4, PACK, 4]),
                op=ALU.mult,
            )
        dt_codes = sbuf("dt_codes", [P, PASSES, Q], U32)
        dt_scales = sbuf("dt_scales", [P, PASSES, Q], U8)
        st_codes = [sbuf("st_codes%d" % h, [P, PASSES, 2 * P], U32, takes_over=("root", "dt_bf")[h]) for h in range(2)]
        st_scales = [sbuf("st_scales%d" % h, [P, PASSES, 2 * P], U8) for h in range(2)]

        def quantize_rows(h):
            nc.vector.quantize_mx(
                out=st_codes[h][:].rearrange("p g f -> p (g f)").bitcast(FP8X4),
                scales=st_scales[h][:].rearrange("p g f -> p (g f)"),
                in_=st_words[h][:].rearrange("p g c f u -> p (g c f u)").bitcast(BF16),
            )

        quantize_rows(0)
        nc.vector.quantize_mx(
            out=dt_codes[:].rearrange("p g q -> p (g q)").bitcast(FP8X4),
            scales=dt_scales[:].rearrange("p g q -> p (g q)"),
            in_=dt_bf[:].rearrange("p g q t -> p (g q t)"),
        )
        quantize_rows(1)

        for h in range(2):
            acc = ps.tile([P, 2 * P], F32, name="acc%d" % h, tag=("bank2", "bank0")[h])
            for g in range(PASSES):
                nc.tensor.matmul_mx(
                    out=acc[:],
                    lhsT=dt_codes[:, g].bitcast(FP8X4),
                    lhsT_scale=dt_scales[:, g],
                    rhs=st_codes[h][:, g].bitcast(FP8X4),
                    rhs_scale=st_scales[h][:, g],
                    start=(g == 0),
                    stop=(g == PASSES - 1),
                )
            cols = slice(h * 2 * P, (h + 1) * 2 * P)
            result = sbuf("result%d" % h, [P, 2 * P], F32)
            nc.vector.tensor_tensor(out=result[:], in0=acc[:], in1=res_sb[:, cols], op=ALU.add)
            nc.sync.dma_start(out[:, cols], result[:])
